import numpy as np
import ml_dtypes


def mxq(x, axis, fmt="e4m3"):
    dtype, down = {"e4m3": (ml_dtypes.float8_e4m3fn, 7), "e5m2": (ml_dtypes.float8_e5m2, 14)}[fmt]
    v = np.moveaxis(np.asarray(x, np.float32).astype(ml_dtypes.bfloat16).astype(np.float64), axis, -1)
    blocks = v.reshape(v.shape[:-1] + (-1, 32))
    amax = np.abs(blocks).max(-1, keepdims=True)
    byte = np.maximum(np.where(amax > 0, np.frexp(amax)[1] - 1 + 127, 0) - down, 1)
    scale = np.exp2(byte - 127.0)
    codes = (blocks / scale).astype(np.float32).astype(dtype).astype(np.float64)
    return np.moveaxis((codes * scale).reshape(v.shape), -1, axis)


WIDE = False


def mx_kscale(k):
    if not WIDE:
        return np.ones(k)
    levels = np.array([10, -10, 5, -5, 0])
    if k % 512:
        return np.exp2(np.random.permutation(np.resize(levels, k // 32))).repeat(32)
    a = np.empty((k // 512, 16))
    for p in range(k // 512):
        a[p, :8] = np.random.permutation(np.resize(levels, 8))
        for g in range(8):
            far = levels[np.abs(levels - a[p, g]) >= 10]
            a[p, g + 8] = far[np.random.randint(len(far))]
    return np.exp2(a.ravel()).repeat(32)


def f64(x):
    return np.asarray(x).astype(np.float64)


def striped(idx):
    return np.tile(idx.reshape(-1, 16).T, (8, 1)).astype(np.uint16)


def unstriped(offs):
    return offs[:16].T.reshape(-1).astype(np.int64)


def striped8(idx):
    return np.concatenate([x.reshape(-1, 16).T for x in idx]).astype(np.uint16)


def runs(offs, k):
    lists = np.stack([offs[16 * r : 16 * r + 16].T.reshape(-1) for r in range(8)]).astype(np.int64)
    return lists[np.arange(k) % 512 // 64]


def pack_weight(w):
    k, n = w.shape
    w = f64(np.asarray(w, np.float32).astype(ml_dtypes.bfloat16)).reshape(k // 32, 32, n)
    amax = np.abs(w).max(1)
    byte = np.clip(np.where(amax > 0, np.frexp(amax)[1] - 1 + 127 - 7, 1), 1, 254)
    scaled = (w * np.exp2(127.0 - byte)[:, None, :]).reshape(k, n).astype(np.float32)
    words = np.ascontiguousarray(scaled.reshape(k // 512, 128, 4, n).transpose(0, 1, 3, 2)).astype(ml_dtypes.float8_e4m3fn).view(np.uint8)
    return words, np.ascontiguousarray(byte.astype(np.uint8).reshape(k // 512, 16, n))


def unpack_weight(words, scales):
    g, p, n, _ = words.shape
    vals = np.ascontiguousarray(words).view(ml_dtypes.float8_e4m3fn).astype(np.float64) * np.repeat(np.exp2(scales.astype(np.float64) - 127.0), 8, axis=1)[..., None]
    return vals.transpose(0, 1, 3, 2).reshape(g * 512, n)


def sigmoid(v):
    return 1.0 / (1.0 + np.exp(-np.maximum(v, -700.0)))


K, T, S, N, G, H = 512, 1024, 512, 512, 2048, 512


def setup_inputs():
    n = np.random.standard_normal
    s = mx_kscale(K)[:, None]
    u = mx_kscale(S)
    packed_xT = pack_weight(n((K, T)) * s)
    packed_dT = pack_weight(n((K, G)) / s)
    return {
        "x_words": packed_xT[0],
        "x_scales": packed_xT[1],
        "d_words": packed_dT[0],
        "d_scales": packed_dT[1],
        "sl": np.random.uniform(1.0, 2.0, (H, 1)).astype(np.float32),
        "th": (0.5 * n((H, 1))).astype(np.float32),
        "gn": (np.random.uniform(0.5, 1.5, (H, 1)) * u[:, None]).astype(np.float32),
        "w1": (n((H, N)) / np.sqrt(2 * H) / u[:, None]).astype(np.float32),
        "w2": (n((K, N)) / np.sqrt(2 * K) / s).astype(np.float32),
        "tau": np.random.uniform(0.3, 0.9, (N, 1)).astype(np.float32),
        "offs": striped(np.random.permutation(T)[:S]),
        "k1": striped8(np.random.randint(0, G, (8, H))),
        "n1": striped(np.random.permutation(S)),
        "n2": striped(np.random.permutation(S)),
        "two": striped(np.random.permutation(T)[:S]),
        "n3": striped(np.random.permutation(S)),
        "n4": striped(np.random.permutation(S)),
    }


def reference(x_words, x_scales, d_words, d_scales, sl, th, gn, w1, w2, tau, offs, k1, n1, n2, two, n3, n4):
    d_k1 = unpack_weight(d_words, d_scales)[np.arange(K)[:, None], runs(k1, K)]
    xq = unpack_weight(x_words, x_scales)[:, unstriped(offs)]
    h = 0.0625 * (d_k1.T @ xq)
    sg = sigmoid(f64(sl) * (h[:, unstriped(n1)] - f64(th)))
    z = f64(gn) * (np.maximum(h * sg, 0.75 * h[:, unstriped(n2)]))
    x_two = unpack_weight(x_words, x_scales)[:, unstriped(two)]
    h2 = mxq(f64(w1), 0, "e4m3").T @ mxq(z, 0, "e4m3") + mxq(f64(w2), 0, "e4m3").T @ x_two
    top = h2.max(axis=1, keepdims=True)
    ea = np.exp(f64(tau) * (h2[:, unstriped(n4)] - top))
    return (0.5 * (h2 - h2[:, unstriped(n3)])) / (ea + 0.25)

@@ -1,0 +1,234 @@
+from contextlib import ExitStack
+
+import concourse.mybir as mybir
+
+F32 = mybir.dt.float32
+BF16 = mybir.dt.bfloat16
+I32 = mybir.dt.int32
+U32 = mybir.dt.uint32
+U16 = mybir.dt.uint16
+U8 = mybir.dt.uint8
+FP8X4 = mybir.dt.float8_e4m3fn_x4
+ALU = mybir.AluOpType
+ACT = mybir.ActivationFunctionType
+
+P = 128
+PACK = 4
+T, G, S = 1024, 2048, 512
+HALF = S // 2
+FLOPS = 3 * 2 * 512 * 512 * 512
+
+
+def tile_picked_pqmixemoera_none_p_kernel(tc, x_words, x_scales, d_words, d_scales, sl, th, gn, w1, w2, tau, offs, k1, n1, n2, two, n3, n4, out):
+    nc = tc.nc
+    with ExitStack() as ctx:
+        keep = ctx.enter_context(tc.tile_pool(name="keep", bufs=1))
+        ring = ctx.enter_context(tc.tile_pool(name="ring", bufs=8))
+        psum = ctx.enter_context(tc.psum_pool(name="psum", bufs=1))
+
+        def load_list(name, src):
+            tile = keep.tile([P, S // 16], U16, name=name)
+            nc.sync.dma_start(tile[:], src)
+            return tile
+
+        def half_of(lst, hf):
+            return lst[:, hf * (HALF // 16) : (hf + 1) * (HALF // 16)]
+
+        def cols(hf):
+            return slice(hf * HALF, (hf + 1) * HALF)
+
+        d_bytes = keep.tile([P, G], U8, name="d_bytes")
+        x_bytes = keep.tile([P, T], U8, name="x_bytes")
+        d_plane = keep.tile([P, S], U8, name="d_plane", align_bytes=64)
+        nc.gpsimd.memset(d_plane[:].bitcast(I32), 0)
+
+        k1_list = load_list("k1_list", k1)
+        nc.sync.dma_start(d_bytes[:].bitcast(I32), d_scales[0].bitcast(I32).unsqueeze(1).to_broadcast([16, 8, G // 4]))
+        offs_list = load_list("offs_list", offs)
+        for q in range(4):
+            nc.sync.dma_start(x_bytes[32 * q : 32 * q + 32, :].bitcast(I32), x_scales[0, 4 * q : 4 * q + 4, :].bitcast(I32).unsqueeze(0).to_broadcast([8, 4, T // 4]))
+        d_table = keep.tile([P, G], U32, name="d_table")
+        nc.sync.dma_start(d_table[:].bitcast(I32), d_words[0].rearrange("p n t -> p (n t)").bitcast(I32))
+        x_table = keep.tile([P, T], U32, name="x_table")
+        nc.sync.dma_start(x_table[:].bitcast(I32), x_words[0].rearrange("p n t -> p (n t)").bitcast(I32))
+        two_list = load_list("two_list", two)
+        n1_list = load_list("n1_list", n1)
+        n2_list = load_list("n2_list", n2)
+        n4_list = load_list("n4_list", n4)
+        n3_list = load_list("n3_list", n3)
+
+        sl_t = keep.tile([P, PACK], F32, name="sl_t")
+        th_t = keep.tile([P, PACK], F32, name="th_t")
+        gn_t = keep.tile([P, PACK], F32, name="gn_t")
+        tau_t = keep.tile([P, PACK], F32, name="tau_t")
+        nc.gpsimd.dma_start(sl_t[:], sl.rearrange("(p t) o -> p (t o)", t=PACK))
+        nc.gpsimd.dma_start(th_t[:], th.rearrange("(p t) o -> p (t o)", t=PACK))
+        nc.gpsimd.dma_start(gn_t[:], gn.rearrange("(p t) o -> p (t o)", t=PACK))
+        with nc.allow_non_contiguous_dma(reason="one value a partition"):
+            nc.gpsimd.dma_start(tau_t[:], tau.rearrange("(t p) o -> p (t o)", p=P))
+
+        d_bytes_picked = keep.tile([P, S], U8, name="d_bytes_picked", tag="staged")
+        nc.vector.tensor_copy(d_bytes_picked[:], d_bytes[:].indirect(k1_list[:]))
+        d_bytes_dealt = keep.tile([P, PACK, P], U8, name="d_bytes_dealt")
+        nc.vector.tensor_copy(d_bytes_dealt[:].rearrange("p t m -> p m t"), d_bytes_picked[:].rearrange("p (m t) -> p m t", t=PACK))
+        for r in range(4):
+            nc.sync.dma_start(d_plane[r:P:32, :].bitcast(I32), d_bytes_dealt[8 * r : P : 32].rearrange("p t m -> p (t m)").bitcast(I32))
+
+        staged = keep.tile([P, 4, PACK, HALF], F32, name="staged", tag="staged")
+        raw = {}
+        for i, (name, w, hf) in enumerate((("w2", w2, 0), ("w2", w2, 1), ("w1", w1, 0), ("w1", w1, 1))):
+            raw[name, hf] = staged[:, i, :, :]
+            nc.sync.dma_start(raw[name, hf], w[:, cols(hf)].rearrange("(p j) c -> p j c", j=PACK))
+
+        xq_plane = keep.tile([P, S], U8, name="xq_plane", align_bytes=64)
+        nc.vector.tensor_copy(xq_plane[:], x_bytes[:].indirect(offs_list[:]))
+        d_picked = keep.tile([P, S], U32, name="d_picked")
+        nc.vector.tensor_copy(d_picked[:], d_table[:].indirect(k1_list[:]))
+        d_codes = keep.tile([P, PACK, P], U32, name="d_codes", align_bytes=64)
+        nc.vector.tensor_copy(d_codes[:].rearrange("p t m -> p m t"), d_picked[:].rearrange("p (m t) -> p m t", t=PACK))
+        xq_codes = [keep.tile([P, HALF], U32, name=f"xq_codes{hf}", align_bytes=64) for hf in range(2)]
+        for hf in range(2):
+            nc.vector.tensor_copy(xq_codes[hf][:], x_table[:].indirect(half_of(offs_list, hf)))
+
+        sig_bias = keep.tile([P, PACK], F32, name="sig_bias")
+        neg_th = keep.tile([P, PACK], F32, name="neg_th")
+        nc.gpsimd.tensor_scalar(neg_th[:], th_t[:], -1.0, 0.0, ALU.mult, ALU.add)
+        nc.gpsimd.tensor_tensor(sig_bias[:], sl_t[:], neg_th[:], ALU.mult)
+        neg_tau = keep.tile([P, PACK], F32, name="neg_tau")
+        nc.gpsimd.tensor_scalar(neg_tau[:], tau_t[:], -1.0, 0.0, ALU.mult, ALU.add)
+
+        h_bank = [psum.tile([P, S], F32, name=f"h_bank{t}") for t in range(PACK)]
+        for t in range(PACK):
+            for hf in range(2):
+                nc.tensor.matmul_mx(
+                    out=h_bank[t][:, cols(hf)],
+                    lhsT=d_codes[:, t, :].bitcast(FP8X4),
+                    lhsT_scale=d_plane[:, t * P : (t + 1) * P],
+                    rhs=xq_codes[hf][:].bitcast(FP8X4),
+                    rhs_scale=xq_plane[:, cols(hf)],
+                    start=True,
+                    stop=True,
+                )
+
+        two_plane = keep.tile([P, S], U8, name="two_plane", align_bytes=64)
+        nc.vector.tensor_copy(two_plane[:], x_bytes[:].indirect(two_list[:]))
+        two_codes = keep.tile([P, S], U32, name="two_codes", align_bytes=64)
+        nc.vector.tensor_copy(two_codes[:], x_table[:].indirect(two_list[:]))
+
+        def woven(flat):
+            return flat.rearrange("p (c i) t -> p c t i", i=4)
+
+        def by_fours(planes):
+            return planes.rearrange("p t (c i) -> p c t i", i=4)
+
+        w_bf, w_codes, w_plane = {}, {}, {}
+        for name in ("w2", "w1"):
+            w_codes[name] = keep.tile([P, S], U32, name=f"{name}_codes", align_bytes=64)
+            w_plane[name] = keep.tile([P, S], U8, name=f"{name}_plane", align_bytes=64)
+            for hf in range(2):
+                w_bf[name, hf] = keep.tile([P, HALF, PACK], BF16, name=f"{name}_bf{hf}", align_bytes=64)
+
+        def cast_w(name, hf, engine):
+            dst, src = woven(w_bf[name, hf][:]), by_fours(raw[name, hf])
+            if engine == "scalar":
+                nc.scalar.copy(dst, src)
+            elif engine == "gpsimd":
+                nc.gpsimd.tensor_scalar(dst, src, 1.0, 0.0, ALU.mult, ALU.add)
+            else:
+                nc.vector.tensor_copy(dst, src)
+
+        def quantize_w(name, hf):
+            nc.vector.quantize_mx(
+                out=w_codes[name][:, cols(hf)].bitcast(FP8X4),
+                scales=w_plane[name][:, cols(hf)],
+                in_=w_bf[name, hf][:].rearrange("p c t -> p (c t)"),
+            )
+
+
+        h_rows = [keep.tile([P, S], F32, name=f"h_rows{t}") for t in range(PACK)]
+        z_planes = [keep.tile([P, PACK, HALF], BF16, name=f"z_planes{hf}") for hf in range(2)]
+        z_woven = [keep.tile([P, HALF, PACK], BF16, name=f"z_woven{hf}", align_bytes=64) for hf in range(2)]
+        z_codes = [keep.tile([P, HALF], U32, name=f"z_codes{hf}", align_bytes=64) for hf in range(2)]
+        z_plane = [keep.tile([P, HALF], U8, name=f"z_plane{hf}", align_bytes=64) for hf in range(2)]
+        h2_bank = [psum.tile([P, S], F32, name=f"h2_bank{m}") for m in range(PACK)]
+
+        def z_piece(t, hf):
+            sg = ring.tile([P, HALF], F32, name="sg")
+            nc.scalar.activation(sg[:], h_rows[t][:].indirect(half_of(n1_list, hf)), ACT.Sigmoid, bias=sig_bias[:, t : t + 1], scale=sl_t[:, t : t + 1])
+            h_n2 = ring.tile([P, HALF], F32, name="h_n2")
+            nc.scalar.activation(h_n2[:], h_rows[t][:].indirect(half_of(n2_list, hf)), ACT.Copy)
+            gated = ring.tile([P, HALF], F32, name="gated")
+            nc.vector.scalar_tensor_tensor(gated[:], h_bank[t][:, cols(hf)], 0.0625, sg[:], ALU.mult, ALU.mult)
+            larger = ring.tile([P, HALF], F32, name="larger")
+            nc.vector.scalar_tensor_tensor(larger[:], h_n2[:], 0.75, gated[:], ALU.mult, ALU.max)
+            nc.vector.tensor_scalar(z_planes[hf][:, t, :], larger[:], gn_t[:, t : t + 1], None, ALU.mult)
+
+        def z_finish(hf):
+            nc.vector.tensor_copy(woven(z_woven[hf][:]), by_fours(z_planes[hf][:]))
+            nc.vector.quantize_mx(out=z_codes[hf][:].bitcast(FP8X4), scales=z_plane[hf][:], in_=z_woven[hf][:].rearrange("p c t -> p (c t)"))
+            for m in range(PACK):
+                nc.tensor.matmul_mx(
+                    out=h2_bank[m][:, cols(hf)],
+                    lhsT=w_codes["w1"][:, m * P : (m + 1) * P].bitcast(FP8X4),
+                    lhsT_scale=w_plane["w1"][:, m * P : (m + 1) * P],
+                    rhs=z_codes[hf][:].bitcast(FP8X4),
+                    rhs_scale=z_plane[hf][:],
+                    start=False,
+                    stop=(hf == 1),
+                )
+
+        for t in range(PACK):
+            if t == 0:
+                nc.vector.tensor_scalar(h_rows[t][:], h_bank[t][:], 0.0625, None, ALU.mult)
+                cast_w("w2", 0, "vector")
+                cast_w("w2", 1, "vector")
+            else:
+                nc.scalar.activation(h_rows[t][:], h_bank[t][:], ACT.Copy, scale=0.0625)
+            z_piece(t, 0)
+            if t < 2:
+                quantize_w("w2", t)
+        for m in range(PACK):
+            nc.tensor.matmul_mx(
+                out=h2_bank[m][:],
+                lhsT=w_codes["w2"][:, m * P : (m + 1) * P].bitcast(FP8X4),
+                lhsT_scale=w_plane["w2"][:, m * P : (m + 1) * P],
+                rhs=two_codes[:].bitcast(FP8X4),
+                rhs_scale=two_plane[:],
+                start=True,
+                stop=False,
+            )
+        cast_w("w1", 0, "vector")
+        cast_w("w1", 1, "vector")
+        quantize_w("w1", 0)
+        quantize_w("w1", 1)
+        z_finish(0)
+        for t in range(PACK):
+            z_piece(t, 1)
+        z_finish(1)
+
+        h2_rows = [keep.tile([P, S], F32, name=f"h2_rows{m}") for m in range(PACK)]
+        top = keep.tile([P, PACK], F32, name="top")
+        exp_bias = keep.tile([P, PACK], F32, name="exp_bias")
+        ea = [keep.tile([P, S], F32, name=f"ea{m}") for m in range(PACK)]
+        den_sq = keep.tile([P, PACK, S], F32, name="den_sq")
+        diff = keep.tile([P, PACK, S], F32, name="diff")
+        for m in range(PACK):
+            nc.vector.tensor_scalar(h2_rows[m][:], h2_bank[m][:], 1.0, None, ALU.mult, ALU.max, accum_out=top[:, m : m + 1])
+            nc.vector.tensor_tensor(exp_bias[:, m : m + 1], top[:, m : m + 1], neg_tau[:, m : m + 1], ALU.mult)
+        for m in range(PACK):
+            for hf in range(2):
+                nc.scalar.activation(ea[m][:, cols(hf)], h2_rows[m][:].indirect(half_of(n4_list, hf)), ACT.Exp, bias=exp_bias[:, m : m + 1], scale=tau_t[:, m : m + 1])
+            nc.scalar.activation(den_sq[:, m, :], ea[m][:], ACT.Square, bias=0.5, scale=2.0)
+        for m in range(PACK):
+            h2_n3 = ring.tile([P, S], F32, name="h2_n3")
+            for hf in range(2):
+                nc.vector.tensor_copy(h2_n3[:, cols(hf)], h2_rows[m][:].indirect(half_of(n3_list, hf)))
+            nc.vector.tensor_tensor(diff[:, m, :], h2_bank[m][:], h2_n3[:], ALU.subtract)
+        out_rows = out.rearrange("(m p) j -> p m j", p=P)
+        for q in range(4):
+            part = slice(q * P, (q + 1) * P)
+            inv = ring.tile([P, PACK, P], F32, name="inv")
+            nc.scalar.activation(inv[:], den_sq[:, :, part], ACT.Abs_reciprocal_sqrt)
+            res = ring.tile([P, PACK, P], F32, name="res")
+            nc.vector.tensor_tensor(res[:], diff[:, :, part], inv[:], ALU.mult)
+            nc.sync.dma_start(out_rows[:, :, part], res[:])

@@ -86,7 +86,7 @@ def tile_picked_pqmixemoera_none_p_kernel(tc, x_words, x_scales, d_words, d_scal
         nc.vector.tensor_copy(d_picked[:], d_table[:].indirect(k1_list[:]))
         d_codes = keep.tile([P, PACK, P], U32, name="d_codes", align_bytes=64)
         nc.vector.tensor_copy(d_codes[:].rearrange("p t m -> p m t"), d_picked[:].rearrange("p (m t) -> p m t", t=PACK))
-        xq_codes = [keep.tile([P, HALF], U32, name=f"xq_codes{hf}", align_bytes=64) for hf in range(2)]
+        xq_codes = [keep.tile([P, HALF], U32, name=f"xq_codes{hf}", tag=f"x_codes{hf}", align_bytes=64) for hf in range(2)]
         for hf in range(2):
             nc.vector.tensor_copy(xq_codes[hf][:], x_table[:].indirect(half_of(offs_list, hf)))
 
@@ -112,8 +112,6 @@ def tile_picked_pqmixemoera_none_p_kernel(tc, x_words, x_scales, d_words, d_scal
 
         two_plane = keep.tile([P, S], U8, name="two_plane", align_bytes=64)
         nc.vector.tensor_copy(two_plane[:], x_bytes[:].indirect(two_list[:]))
-        two_codes = keep.tile([P, S], U32, name="two_codes", align_bytes=64)
-        nc.vector.tensor_copy(two_codes[:], x_table[:].indirect(two_list[:]))
 
         def woven(flat):
             return flat.rearrange("p (c i) t -> p c t i", i=4)
@@ -133,7 +131,7 @@ def tile_picked_pqmixemoera_none_p_kernel(tc, x_words, x_scales, d_words, d_scal
             if engine == "scalar":
                 nc.scalar.copy(dst, src)
             elif engine == "gpsimd":
-                nc.gpsimd.tensor_scalar(dst, src, 1.0, 0.0, ALU.mult, ALU.add)
+                nc.gpsimd.tensor_scalar(w_bf[name, hf][:], raw[name, hf].rearrange("p t c -> p c t"), 1.0, 0.0, ALU.mult, ALU.add)
             else:
                 nc.vector.tensor_copy(dst, src)
 
@@ -144,6 +142,10 @@ def tile_picked_pqmixemoera_none_p_kernel(tc, x_words, x_scales, d_words, d_scal
                 in_=w_bf[name, hf][:].rearrange("p c t -> p (c t)"),
             )
 
+
+        for name in ("w2", "w1"):
+            for hf in range(2):
+                cast_w(name, hf, "gpsimd")
 
         h_rows = [keep.tile([P, S], F32, name=f"h_rows{t}") for t in range(PACK)]
         z_planes = [keep.tile([P, PACK, HALF], BF16, name=f"z_planes{hf}") for hf in range(2)]
@@ -178,12 +180,10 @@ def tile_picked_pqmixemoera_none_p_kernel(tc, x_words, x_scales, d_words, d_scal
                 )
 
         for t in range(PACK):
-            if t == 0:
-                nc.vector.tensor_scalar(h_rows[t][:], h_bank[t][:], 0.0625, None, ALU.mult)
-                cast_w("w2", 0, "vector")
-                cast_w("w2", 1, "vector")
-            else:
-                nc.scalar.activation(h_rows[t][:], h_bank[t][:], ACT.Copy, scale=0.0625)
+            nc.vector.tensor_scalar(h_rows[t][:], h_bank[t][:], 0.0625, None, ALU.mult)
+        two_codes = keep.tile([P, S], U32, name="two_codes", tag="x_codes1", align_bytes=64)
+        nc.vector.tensor_copy(two_codes[:], x_table[:].indirect(two_list[:]))
+        for t in range(PACK):
             z_piece(t, 0)
             if t < 2:
                 quantize_w("w2", t)
@@ -197,8 +197,6 @@ def tile_picked_pqmixemoera_none_p_kernel(tc, x_words, x_scales, d_words, d_scal
                 start=True,
                 stop=False,
             )
-        cast_w("w1", 0, "vector")
-        cast_w("w1", 1, "vector")
         quantize_w("w1", 0)
         quantize_w("w1", 1)
         z_finish(0)
@@ -207,17 +205,17 @@ def tile_picked_pqmixemoera_none_p_kernel(tc, x_words, x_scales, d_words, d_scal
         z_finish(1)
 
         h2_rows = [keep.tile([P, S], F32, name=f"h2_rows{m}") for m in range(PACK)]
-        top = keep.tile([P, PACK], F32, name="top")
-        exp_bias = keep.tile([P, PACK], F32, name="exp_bias")
+        top = [keep.tile([P, 1], F32, name=f"top{m}") for m in range(PACK)]
+        exp_bias = [keep.tile([P, 1], F32, name=f"exp_bias{m}") for m in range(PACK)]
         ea = [keep.tile([P, S], F32, name=f"ea{m}") for m in range(PACK)]
         den_sq = keep.tile([P, PACK, S], F32, name="den_sq")
         diff = keep.tile([P, PACK, S], F32, name="diff")
         for m in range(PACK):
-            nc.vector.tensor_scalar(h2_rows[m][:], h2_bank[m][:], 1.0, None, ALU.mult, ALU.max, accum_out=top[:, m : m + 1])
-            nc.vector.tensor_tensor(exp_bias[:, m : m + 1], top[:, m : m + 1], neg_tau[:, m : m + 1], ALU.mult)
+            nc.vector.tensor_scalar(h2_rows[m][:], h2_bank[m][:], 1.0, None, ALU.mult, ALU.max, accum_out=top[m][:])
+            nc.gpsimd.tensor_tensor(exp_bias[m][:], top[m][:], neg_tau[:, m : m + 1], ALU.mult)
         for m in range(PACK):
             for hf in range(2):
-                nc.scalar.activation(ea[m][:, cols(hf)], h2_rows[m][:].indirect(half_of(n4_list, hf)), ACT.Exp, bias=exp_bias[:, m : m + 1], scale=tau_t[:, m : m + 1])
+                nc.scalar.activation(ea[m][:, cols(hf)], h2_rows[m][:].indirect(half_of(n4_list, hf)), ACT.Exp, bias=exp_bias[m][:], scale=tau_t[:, m : m + 1])
             nc.scalar.activation(den_sq[:, m, :], ea[m][:], ACT.Square, bias=0.5, scale=2.0)
         for m in range(PACK):
             h2_n3 = ring.tile([P, S], F32, name="h2_n3")

from contextlib import ExitStack

import concourse.mybir as mybir

F32 = mybir.dt.float32
BF16 = mybir.dt.bfloat16
I32 = mybir.dt.int32
U32 = mybir.dt.uint32
U16 = mybir.dt.uint16
U8 = mybir.dt.uint8
FP8X4 = mybir.dt.float8_e4m3fn_x4
ALU = mybir.AluOpType
ACT = mybir.ActivationFunctionType

P = 128
PACK = 4
T, G, S = 1024, 2048, 512
HALF = S // 2
FLOPS = 3 * 2 * 512 * 512 * 512


def tile_picked_pqmixemoera_none_p_kernel(tc, x_words, x_scales, d_words, d_scales, sl, th, gn, w1, w2, tau, offs, k1, n1, n2, two, n3, n4, out):
    nc = tc.nc
    with ExitStack() as ctx:
        keep = ctx.enter_context(tc.tile_pool(name="keep", bufs=1))
        ring = ctx.enter_context(tc.tile_pool(name="ring", bufs=8))
        psum = ctx.enter_context(tc.psum_pool(name="psum", bufs=1))

        def load_list(name, src):
            tile = keep.tile([P, S // 16], U16, name=name)
            nc.sync.dma_start(tile[:], src)
            return tile

        def half_of(lst, hf):
            return lst[:, hf * (HALF // 16) : (hf + 1) * (HALF // 16)]

        def cols(hf):
            return slice(hf * HALF, (hf + 1) * HALF)

        d_bytes = keep.tile([P, G], U8, name="d_bytes")
        x_bytes = keep.tile([P, T], U8, name="x_bytes")
        d_plane = keep.tile([P, S], U8, name="d_plane", align_bytes=64)
        nc.gpsimd.memset(d_plane[:].bitcast(I32), 0)

        k1_list = load_list("k1_list", k1)
        nc.sync.dma_start(d_bytes[:].bitcast(I32), d_scales[0].bitcast(I32).unsqueeze(1).to_broadcast([16, 8, G // 4]))
        offs_list = load_list("offs_list", offs)
        for q in range(4):
            nc.sync.dma_start(x_bytes[32 * q : 32 * q + 32, :].bitcast(I32), x_scales[0, 4 * q : 4 * q + 4, :].bitcast(I32).unsqueeze(0).to_broadcast([8, 4, T // 4]))
        d_table = keep.tile([P, G], U32, name="d_table")
        nc.sync.dma_start(d_table[:].bitcast(I32), d_words[0].rearrange("p n t -> p (n t)").bitcast(I32))
        x_table = keep.tile([P, T], U32, name="x_table")
        nc.sync.dma_start(x_table[:].bitcast(I32), x_words[0].rearrange("p n t -> p (n t)").bitcast(I32))
        two_list = load_list("two_list", two)
        n1_list = load_list("n1_list", n1)
        n2_list = load_list("n2_list", n2)
        n4_list = load_list("n4_list", n4)
        n3_list = load_list("n3_list", n3)

        sl_t = keep.tile([P, PACK], F32, name="sl_t")
        th_t = keep.tile([P, PACK], F32, name="th_t")
        gn_t = keep.tile([P, PACK], F32, name="gn_t")
        tau_t = keep.tile([P, PACK], F32, name="tau_t")
        nc.gpsimd.dma_start(sl_t[:], sl.rearrange("(p t) o -> p (t o)", t=PACK))
        nc.gpsimd.dma_start(th_t[:], th.rearrange("(p t) o -> p (t o)", t=PACK))
        nc.gpsimd.dma_start(gn_t[:], gn.rearrange("(p t) o -> p (t o)", t=PACK))
        with nc.allow_non_contiguous_dma(reason="one value a partition"):
            nc.gpsimd.dma_start(tau_t[:], tau.rearrange("(t p) o -> p (t o)", p=P))

        d_bytes_picked = keep.tile([P, S], U8, name="d_bytes_picked", tag="staged")
        nc.vector.tensor_copy(d_bytes_picked[:], d_bytes[:].indirect(k1_list[:]))
        d_bytes_dealt = keep.tile([P, PACK, P], U8, name="d_bytes_dealt")
        nc.vector.tensor_copy(d_bytes_dealt[:].rearrange("p t m -> p m t"), d_bytes_picked[:].rearrange("p (m t) -> p m t", t=PACK))
        for r in range(4):
            nc.sync.dma_start(d_plane[r:P:32, :].bitcast(I32), d_bytes_dealt[8 * r : P : 32].rearrange("p t m -> p (t m)").bitcast(I32))

        staged = keep.tile([P, 4, PACK, HALF], F32, name="staged", tag="staged")
        raw = {}
        for i, (name, w, hf) in enumerate((("w2", w2, 0), ("w2", w2, 1), ("w1", w1, 0), ("w1", w1, 1))):
            raw[name, hf] = staged[:, i, :, :]
            nc.sync.dma_start(raw[name, hf], w[:, cols(hf)].rearrange("(p j) c -> p j c", j=PACK))

        xq_plane = keep.tile([P, S], U8, name="xq_plane", align_bytes=64)
        nc.vector.tensor_copy(xq_plane[:], x_bytes[:].indirect(offs_list[:]))
        d_picked = keep.tile([P, S], U32, name="d_picked")
        nc.vector.tensor_copy(d_picked[:], d_table[:].indirect(k1_list[:]))
        d_codes = keep.tile([P, PACK, P], U32, name="d_codes", align_bytes=64)
        nc.vector.tensor_copy(d_codes[:].rearrange("p t m -> p m t"), d_picked[:].rearrange("p (m t) -> p m t", t=PACK))
        xq_codes = [keep.tile([P, HALF], U32, name=f"xq_codes{hf}", tag=f"x_codes{hf}", align_bytes=64) for hf in range(2)]
        for hf in range(2):
            nc.vector.tensor_copy(xq_codes[hf][:], x_table[:].indirect(half_of(offs_list, hf)))

        sig_bias = keep.tile([P, PACK], F32, name="sig_bias")
        neg_th = keep.tile([P, PACK], F32, name="neg_th")
        nc.gpsimd.tensor_scalar(neg_th[:], th_t[:], -1.0, 0.0, ALU.mult, ALU.add)
        nc.gpsimd.tensor_tensor(sig_bias[:], sl_t[:], neg_th[:], ALU.mult)
        neg_tau = keep.tile([P, PACK], F32, name="neg_tau")
        nc.gpsimd.tensor_scalar(neg_tau[:], tau_t[:], -1.0, 0.0, ALU.mult, ALU.add)

        h_bank = [psum.tile([P, S], F32, name=f"h_bank{t}") for t in range(PACK)]
        for t in range(PACK):
            for hf in range(2):
                nc.tensor.matmul_mx(
                    out=h_bank[t][:, cols(hf)],
                    lhsT=d_codes[:, t, :].bitcast(FP8X4),
                    lhsT_scale=d_plane[:, t * P : (t + 1) * P],
                    rhs=xq_codes[hf][:].bitcast(FP8X4),
                    rhs_scale=xq_plane[:, cols(hf)],
                    start=True,
                    stop=True,
                )

        two_plane = keep.tile([P, S], U8, name="two_plane", align_bytes=64)
        nc.vector.tensor_copy(two_plane[:], x_bytes[:].indirect(two_list[:]))

        def woven(flat):
            return flat.rearrange("p (c i) t -> p c t i", i=4)

        def by_fours(planes):
            return planes.rearrange("p t (c i) -> p c t i", i=4)

        w_bf, w_codes, w_plane = {}, {}, {}
        for name in ("w2", "w1"):
            w_codes[name] = keep.tile([P, S], U32, name=f"{name}_codes", align_bytes=64)
            w_plane[name] = keep.tile([P, S], U8, name=f"{name}_plane", align_bytes=64)
            for hf in range(2):
                w_bf[name, hf] = keep.tile([P, HALF, PACK], BF16, name=f"{name}_bf{hf}", align_bytes=64)

        def cast_w(name, hf, engine):
            dst, src = woven(w_bf[name, hf][:]), by_fours(raw[name, hf])
            if engine == "scalar":
                nc.scalar.copy(dst, src)
            elif engine == "gpsimd":
                nc.gpsimd.tensor_scalar(w_bf[name, hf][:], raw[name, hf].rearrange("p t c -> p c t"), 1.0, 0.0, ALU.mult, ALU.add)
            else:
                nc.vector.tensor_copy(dst, src)

        def quantize_w(name, hf):
            nc.vector.quantize_mx(
                out=w_codes[name][:, cols(hf)].bitcast(FP8X4),
                scales=w_plane[name][:, cols(hf)],
                in_=w_bf[name, hf][:].rearrange("p c t -> p (c t)"),
            )


        for name in ("w2", "w1"):
            for hf in range(2):
                cast_w(name, hf, "gpsimd")

        h_rows = [keep.tile([P, S], F32, name=f"h_rows{t}") for t in range(PACK)]
        z_planes = [keep.tile([P, PACK, HALF], BF16, name=f"z_planes{hf}") for hf in range(2)]
        z_woven = [keep.tile([P, HALF, PACK], BF16, name=f"z_woven{hf}", align_bytes=64) for hf in range(2)]
        z_codes = [keep.tile([P, HALF], U32, name=f"z_codes{hf}", align_bytes=64) for hf in range(2)]
        z_plane = [keep.tile([P, HALF], U8, name=f"z_plane{hf}", align_bytes=64) for hf in range(2)]
        h2_bank = [psum.tile([P, S], F32, name=f"h2_bank{m}") for m in range(PACK)]

        def z_piece(t, hf):
            sg = ring.tile([P, HALF], F32, name="sg")
            nc.scalar.activation(sg[:], h_rows[t][:].indirect(half_of(n1_list, hf)), ACT.Sigmoid, bias=sig_bias[:, t : t + 1], scale=sl_t[:, t : t + 1])
            h_n2 = ring.tile([P, HALF], F32, name="h_n2")
            nc.scalar.activation(h_n2[:], h_rows[t][:].indirect(half_of(n2_list, hf)), ACT.Copy)
            gated = ring.tile([P, HALF], F32, name="gated")
            nc.vector.scalar_tensor_tensor(gated[:], h_bank[t][:, cols(hf)], 0.0625, sg[:], ALU.mult, ALU.mult)
            larger = ring.tile([P, HALF], F32, name="larger")
            nc.vector.scalar_tensor_tensor(larger[:], h_n2[:], 0.75, gated[:], ALU.mult, ALU.max)
            nc.vector.tensor_scalar(z_planes[hf][:, t, :], larger[:], gn_t[:, t : t + 1], None, ALU.mult)

        def z_finish(hf):
            nc.vector.tensor_copy(woven(z_woven[hf][:]), by_fours(z_planes[hf][:]))
            nc.vector.quantize_mx(out=z_codes[hf][:].bitcast(FP8X4), scales=z_plane[hf][:], in_=z_woven[hf][:].rearrange("p c t -> p (c t)"))
            for m in range(PACK):
                nc.tensor.matmul_mx(
                    out=h2_bank[m][:, cols(hf)],
                    lhsT=w_codes["w1"][:, m * P : (m + 1) * P].bitcast(FP8X4),
                    lhsT_scale=w_plane["w1"][:, m * P : (m + 1) * P],
                    rhs=z_codes[hf][:].bitcast(FP8X4),
                    rhs_scale=z_plane[hf][:],
                    start=False,
                    stop=(hf == 1),
                )

        for t in range(PACK):
            nc.vector.tensor_scalar(h_rows[t][:], h_bank[t][:], 0.0625, None, ALU.mult)
        two_codes = keep.tile([P, S], U32, name="two_codes", tag="x_codes1", align_bytes=64)
        nc.vector.tensor_copy(two_codes[:], x_table[:].indirect(two_list[:]))
        for t in range(PACK):
            z_piece(t, 0)
            if t < 2:
                quantize_w("w2", t)
        for m in range(PACK):
            nc.tensor.matmul_mx(
                out=h2_bank[m][:],
                lhsT=w_codes["w2"][:, m * P : (m + 1) * P].bitcast(FP8X4),
                lhsT_scale=w_plane["w2"][:, m * P : (m + 1) * P],
                rhs=two_codes[:].bitcast(FP8X4),
                rhs_scale=two_plane[:],
                start=True,
                stop=False,
            )
        quantize_w("w1", 0)
        quantize_w("w1", 1)
        z_finish(0)
        for t in range(PACK):
            z_piece(t, 1)
        z_finish(1)

        h2_rows = [keep.tile([P, S], F32, name=f"h2_rows{m}") for m in range(PACK)]
        top = [keep.tile([P, 1], F32, name=f"top{m}") for m in range(PACK)]
        exp_bias = [keep.tile([P, 1], F32, name=f"exp_bias{m}") for m in range(PACK)]
        ea = [keep.tile([P, S], F32, name=f"ea{m}") for m in range(PACK)]
        den_sq = keep.tile([P, PACK, S], F32, name="den_sq")
        diff = keep.tile([P, PACK, S], F32, name="diff")
        for m in range(PACK):
            nc.vector.tensor_scalar(h2_rows[m][:], h2_bank[m][:], 1.0, None, ALU.mult, ALU.max, accum_out=top[m][:])
            nc.gpsimd.tensor_tensor(exp_bias[m][:], top[m][:], neg_tau[:, m : m + 1], ALU.mult)
        for m in range(PACK):
            for hf in range(2):
                nc.scalar.activation(ea[m][:, cols(hf)], h2_rows[m][:].indirect(half_of(n4_list, hf)), ACT.Exp, bias=exp_bias[m][:], scale=tau_t[:, m : m + 1])
            nc.scalar.activation(den_sq[:, m, :], ea[m][:], ACT.Square, bias=0.5, scale=2.0)
        for m in range(PACK):
            h2_n3 = ring.tile([P, S], F32, name="h2_n3")
            for hf in range(2):
                nc.vector.tensor_copy(h2_n3[:, cols(hf)], h2_rows[m][:].indirect(half_of(n3_list, hf)))
            nc.vector.tensor_tensor(diff[:, m, :], h2_bank[m][:], h2_n3[:], ALU.subtract)
        out_rows = out.rearrange("(m p) j -> p m j", p=P)
        for q in range(4):
            part = slice(q * P, (q + 1) * P)
            inv = ring.tile([P, PACK, P], F32, name="inv")
            nc.scalar.activation(inv[:], den_sq[:, :, part], ACT.Abs_reciprocal_sqrt)
            res = ring.tile([P, PACK, P], F32, name="res")
            nc.vector.tensor_tensor(res[:], diff[:, :, part], inv[:], ALU.mult)
            nc.sync.dma_start(out_rows[:, :, part], res[:])
